import numpy as np
import ml_dtypes


def mxq(x, axis, fmt="e4m3"):
    dtype, down = {"e4m3": (ml_dtypes.float8_e4m3fn, 7), "e5m2": (ml_dtypes.float8_e5m2, 14)}[fmt]
    v = np.moveaxis(np.asarray(x, np.float32).astype(ml_dtypes.bfloat16).astype(np.float64), axis, -1)
    blocks = v.reshape(v.shape[:-1] + (-1, 32))
    amax = np.abs(blocks).max(-1, keepdims=True)
    byte = np.maximum(np.where(amax > 0, np.frexp(amax)[1] - 1 + 127, 0) - down, 1)
    scale = np.exp2(byte - 127.0)
    codes = (blocks / scale).astype(np.float32).astype(dtype).astype(np.float64)
    return np.moveaxis((codes * scale).reshape(v.shape), -1, axis)


WIDE = False


def mx_kscale(k):
    if not WIDE:
        return np.ones(k)
    levels = np.array([10, -10, 5, -5, 0])
    if k % 512:
        return np.exp2(np.random.permutation(np.resize(levels, k // 32))).repeat(32)
    a = np.empty((k // 512, 16))
    for p in range(k // 512):
        a[p, :8] = np.random.permutation(np.resize(levels, 8))
        for g in range(8):
            far = levels[np.abs(levels - a[p, g]) >= 10]
            a[p, g + 8] = far[np.random.randint(len(far))]
    return np.exp2(a.ravel()).repeat(32)


def f64(x):
    return np.asarray(x).astype(np.float64)


def striped(idx):
    return np.tile(np.asarray(idx).reshape(-1, 16).T, (8, 1)).astype(np.uint16)


def unstriped(offs):
    return offs[:16].T.reshape(-1).astype(np.int64)


E2M1 = np.array([0.0, 0.5, 1.0, 1.5, 2.0, 3.0, 4.0, 6.0, -0.0, -0.5, -1.0, -1.5, -2.0, -3.0, -4.0, -6.0])


def pack_weight(w, fmt):
    k, n = w.shape
    w = f64(np.asarray(w, np.float32).astype(ml_dtypes.bfloat16)).reshape(k // 32, 32, n)
    amax = np.abs(w).max(1)
    if fmt == "e4m3":
        byte = np.frexp(amax)[1] - 1 + 127 - 7
    else:
        mant, ex = np.frexp(amax / 6.0)
        byte = np.where(mant > 0.5, ex, ex - 1) + 127
    byte = np.clip(np.where(amax > 0, byte, 1), 1, 254)
    scaled = (w * np.exp2(127.0 - byte)[:, None, :]).reshape(k, n).astype(np.float32)
    by_word = np.ascontiguousarray(scaled.reshape(k // 512, 128, 4, n).transpose(0, 1, 3, 2))
    if fmt == "e4m3":
        words = by_word.astype(ml_dtypes.float8_e4m3fn).view(np.uint8)
    else:
        c = by_word.astype(ml_dtypes.float4_e2m1fn).view(np.uint8) & 0xF
        words = (c[..., 0::2] | (c[..., 1::2] << 4)).reshape(k // 512, 128, 2 * n)
    return np.ascontiguousarray(words), np.ascontiguousarray(byte.astype(np.uint8).reshape(k // 512, 16, n))


def unpack_weight(words, scales, fmt):
    g, _, n = scales.shape
    words = np.ascontiguousarray(words).reshape(g, 128, n, -1)
    if fmt == "e4m3":
        vals = words.view(ml_dtypes.float8_e4m3fn).astype(np.float64)
    else:
        nib = np.empty((g, 128, n, 4), np.uint8)
        nib[..., 0::2] = words & 0xF
        nib[..., 1::2] = words >> 4
        vals = E2M1[nib]
    vals = vals * np.repeat(np.exp2(scales.astype(np.float64) - 127.0), 8, axis=1)[..., None]
    return vals.transpose(0, 1, 3, 2).reshape(g * 512, n)


def sigmoid(v):
    return 1.0 / (1.0 + np.exp(-v))


B, N, T, D, NQ = 1, 512, 2048, 1024, 128


def setup_inputs():
    n = np.random.standard_normal
    idx = np.random.permutation(T)[:B * N]
    s = mx_kscale(D)[:, None]
    kp = pack_weight(n((D, T)) / s, "e2m1")
    cp = pack_weight(n((D, T)) / s, "e2m1")
    return {
        "qT": (n((B, D, NQ)) * s * (1.00 / np.sqrt(D))).astype(np.float32),
        "k_words": np.ascontiguousarray(kp[0].reshape(1, 2, 128, T, 2).transpose(0, 2, 3, 1, 4)).reshape(1, 128, T, 4),
        "k_scales": kp[1],
        "c_words": np.ascontiguousarray(cp[0].reshape(1, 2, 128, T, 2).transpose(0, 2, 3, 1, 4)).reshape(1, 128, T, 4),
        "c_scales": cp[1],
        "offs": striped(idx),
    }


def reference(qT, k_words, k_scales, c_words, c_scales, offs):
    idx = unstriped(offs)
    pick = lambda x, which: x[:, which].reshape(x.shape[0], B, -1).transpose(1, 0, 2)
    k = unpack_weight(k_words.reshape(1, 128, T, 2, 2).transpose(0, 3, 1, 2, 4).reshape(2, 128, 2 * T), k_scales, "e2m1")
    kg = pick(k, idx)
    c = unpack_weight(c_words.reshape(1, 128, T, 2, 2).transpose(0, 3, 1, 2, 4).reshape(2, 128, 2 * T), c_scales, "e2m1")
    cg = pick(c, idx)
    qq = mxq(f64(qT), 1, "e4m3")
    a = qq.transpose(0, 2, 1) @ kg
    z = qq.transpose(0, 2, 1) @ cg
    y = sigmoid(a) * z
    return y

@@ -1,0 +1,119 @@
+from contextlib import ExitStack
+
+import concourse.mybir as mybir
+
+N, T, D, NQ = 512, 2048, 1024, 128
+FLOPS = 2 * 2 * NQ * N * D
+
+F32 = mybir.dt.float32
+BF16 = mybir.dt.bfloat16
+I32 = mybir.dt.int32
+U32 = mybir.dt.uint32
+U16 = mybir.dt.uint16
+U8 = mybir.dt.uint8
+FP8X4 = mybir.dt.float8_e4m3fn_x4
+FP4X4 = mybir.dt.float4_e2m1fn_x4
+ACT = mybir.ActivationFunctionType
+ALU = mybir.AluOpType
+
+P = 128
+PACK = 4
+PASSES = 2
+HALF = N // 2
+
+
+def tile_attend_twokey_topk_kernel(tc, qT, k_words, k_scales, c_words, c_scales, offs, out):
+    nc = tc.nc
+    with ExitStack() as ctx:
+        pool = ctx.enter_context(tc.tile_pool(name="held", bufs=1))
+        psum = ctx.enter_context(tc.psum_pool(name="psum", bufs=1))
+
+        offsets = pool.tile([P, N // 16], U16, name="offsets")
+        ks_win = pool.tile([P, T], U8, name="ks_win", align_bytes=64)
+        cs_win = pool.tile([P, T], U8, name="cs_win", align_bytes=64)
+        kw_win = pool.tile([P, T], I32, name="kw_win", align_bytes=64)
+        cw_win = pool.tile([P, T], I32, name="cw_win", align_bytes=64)
+        s_got = pool.tile([P, 2, N], U8, name="s_got", align_bytes=64)
+        planes = pool.tile([P, PASSES, 2, N], U8, name="planes", align_bytes=64)
+        warm = pool.tile([P, 8], F32, name="warm")
+        warm_out = pool.tile([P, 8], F32, name="warm_out")
+
+        def load_scales(win, scales):
+            rows = scales.rearrange("o f t -> f o t")
+            nc.sync.dma_start(out=win[96:P, :].bitcast(I32), in_=rows.bitcast(I32))
+            nc.vector.memset(win[0:96, :].bitcast(I32), 0)
+
+        def load_words(win, words):
+            nc.sync.dma_start(out=win[:], in_=words[0].rearrange("p t b -> p (t b)").bitcast(I32))
+
+        nc.sync.dma_start(offsets[:], offs)
+        load_scales(ks_win, k_scales)
+        load_scales(cs_win, c_scales)
+        q_raw = pool.tile([P, PASSES, PACK, NQ], F32, name="q_raw")
+        nc.sync.dma_start(out=q_raw[:], in_=qT[0].rearrange("(g p j) w -> p g j w", g=PASSES, j=PACK))
+        load_words(kw_win, k_words)
+        load_words(cw_win, c_words)
+        nc.vector.memset(warm[:], 0.0)
+        nc.vector.memset(planes[:].rearrange("p g s n -> p (g s n)").bitcast(I32), 0)
+
+        nc.scalar.activation(warm_out[:], warm[:], ACT.Sigmoid)
+
+        nc.vector.tensor_copy(s_got[:, 0, :], ks_win[:].indirect(offsets[:]))
+        nc.vector.tensor_copy(s_got[:, 1, :], cs_win[:].indirect(offsets[:]))
+        for quad in range(4):
+            nc.scalar.dma_start(
+                out=planes[32 * quad : 32 * quad + 4].rearrange("p g s n -> p g (s n)").bitcast(I32),
+                in_=s_got[96 + 8 * quad : 96 + 8 * quad + 8].rearrange("p s n -> p (s n)").bitcast(I32),
+            )
+
+        kw_got = pool.tile([P, N], U32, name="kw_got", align_bytes=64)
+        kw = pool.tile([P, PASSES, N], U16, name="kw", align_bytes=64)
+        nc.vector.tensor_copy(kw_got[:], kw_win[:].bitcast(U32).indirect(offsets[:]))
+        nc.vector.tensor_copy(kw[:], kw_got[:].bitcast(U16).rearrange("p (n g) -> p g n", g=PASSES))
+
+        q_bf = pool.tile([P, PASSES, NQ, PACK], BF16, name="q_bf", align_bytes=64)
+        q_codes = pool.tile([P, PASSES * NQ], U32, name="q_codes", align_bytes=64)
+        q_scales = pool.tile([P, PASSES * NQ], U8, name="q_scales", align_bytes=64)
+        for g in range(PASSES):
+            nc.scalar.activation(q_bf[:, g], q_raw[:, g].rearrange("p j w -> p w j"), ACT.Copy)
+        nc.vector.quantize_mx(
+            out=q_codes[:].bitcast(FP8X4), scales=q_scales[:], in_=q_bf[:].rearrange("p g w j -> p (g w j)")
+        )
+
+        def product(acc, words, table, cols, wcols):
+            for g in range(PASSES):
+                nc.tensor.matmul_mx(
+                    out=acc,
+                    lhsT=q_codes[:, g * NQ : (g + 1) * NQ].bitcast(FP8X4),
+                    lhsT_scale=q_scales[:, g * NQ : (g + 1) * NQ],
+                    rhs=words[:, g, wcols].bitcast(FP4X4),
+                    rhs_scale=planes[:, g, table, cols],
+                    start=(g == 0),
+                    stop=(g == PASSES - 1),
+                )
+
+        a_ps = psum.tile([P, N], F32, name="a_ps")
+        product(a_ps[:], kw, 0, slice(0, N), slice(0, N))
+        gate = pool.tile([P, N], F32, name="gate")
+        nc.scalar.activation(gate[:], a_ps[:], ACT.Sigmoid)
+
+        z_ps = []
+        for h in range(2):
+            got = pool.tile([P, HALF], U32, name="cw_got%d" % h, align_bytes=64)
+            nc.vector.tensor_copy(got[:], cw_win[:].bitcast(U32).indirect(offsets[:, h * 16 : (h + 1) * 16]))
+            z = psum.tile([P, N], F32, name="z_ps%d" % h)
+            for s in range(2):
+                c0 = h * HALF + s * P
+                if h == 1 or s == 0:
+                    width = P if h == 1 else HALF
+                    cw = pool.tile([P, PASSES, width], U16, name="cw%d%d" % (h, s), align_bytes=64)
+                    src = got[:, s * P : s * P + width].bitcast(U16)
+                    nc.vector.tensor_copy(cw[:], src.rearrange("p (n g) -> p g n", g=PASSES))
+                w0 = 0 if h == 1 else s * P
+                product(z[:, s * P : (s + 1) * P], cw, 1, slice(c0, c0 + P), slice(w0, w0 + P))
+            z_ps.append(z)
+
+        for h in range(2):
+            y = pool.tile([P, HALF], F32, name="y%d" % h)
+            nc.vector.tensor_tensor(y[:], z_ps[h][:, 0:HALF], gate[:, h * HALF : (h + 1) * HALF], ALU.mult)
+            nc.sync.dma_start(out=out[0][:, h * HALF : (h + 1) * HALF], in_=y[:])

@@ -29,42 +29,54 @@ def tile_attend_twokey_topk_kernel(tc, qT, k_words, k_scales, c_words, c_scales,
         psum = ctx.enter_context(tc.psum_pool(name="psum", bufs=1))
 
         offsets = pool.tile([P, N // 16], U16, name="offsets")
-        ks_win = pool.tile([P, T], U8, name="ks_win", align_bytes=64)
+        ks_win = pool.tile([P, T], U8, name="ks_win", tag="ks_then_cw", align_bytes=64)
         cs_win = pool.tile([P, T], U8, name="cs_win", align_bytes=64)
         kw_win = pool.tile([P, T], I32, name="kw_win", align_bytes=64)
-        cw_win = pool.tile([P, T], I32, name="cw_win", align_bytes=64)
-        s_got = pool.tile([P, 2, N], U8, name="s_got", align_bytes=64)
-        planes = pool.tile([P, PASSES, 2, N], U8, name="planes", align_bytes=64)
+        ks_got = pool.tile([P, N], U8, name="ks_got", align_bytes=64)
+        cs_got = pool.tile([P, N], U8, name="cs_got", align_bytes=64)
+        k_planes = pool.tile([P, PASSES, N], U8, name="k_planes", align_bytes=64)
+        c_planes = pool.tile([P, PASSES, N], U8, name="c_planes", align_bytes=64)
         warm = pool.tile([P, 8], F32, name="warm")
         warm_out = pool.tile([P, 8], F32, name="warm_out")
 
-        def load_scales(win, scales):
+        def load_scales(win, scales, first, blanks, engine):
             rows = scales.rearrange("o f t -> f o t")
-            nc.sync.dma_start(out=win[96:P, :].bitcast(I32), in_=rows.bitcast(I32))
-            nc.vector.memset(win[0:96, :].bitcast(I32), 0)
+            nc.sync.dma_start(out=win[first : first + 32, :].bitcast(I32), in_=rows.bitcast(I32))
+            for lo, hi in blanks:
+                engine.memset(win[lo:hi, :].bitcast(I32), 0)
+
+        def place(queue, planes, got, first, quad):
+            queue.dma_start(
+                out=planes[32 * quad : 32 * quad + 4].bitcast(I32),
+                in_=got[first + 8 * quad : first + 8 * quad + 8].bitcast(I32),
+            )
 
         def load_words(win, words):
             nc.sync.dma_start(out=win[:], in_=words[0].rearrange("p t b -> p (t b)").bitcast(I32))
 
         nc.sync.dma_start(offsets[:], offs)
-        load_scales(ks_win, k_scales)
-        load_scales(cs_win, c_scales)
-        q_raw = pool.tile([P, PASSES, PACK, NQ], F32, name="q_raw")
-        nc.sync.dma_start(out=q_raw[:], in_=qT[0].rearrange("(g p j) w -> p g j w", g=PASSES, j=PACK))
+        load_scales(ks_win, k_scales, 96, [(0, 96)], nc.vector)
+        load_scales(cs_win, c_scales, 32, [(0, 32), (64, P)], nc.gpsimd)
         load_words(kw_win, k_words)
-        load_words(cw_win, c_words)
+        q_raw = []
+        for g in range(PASSES):
+            raw = pool.tile([P, PACK, NQ], F32, name="q_raw%d" % g)
+            nc.sync.dma_start(out=raw[:], in_=qT[0].rearrange("(g p j) w -> g p j w", g=PASSES, j=PACK)[g])
+            q_raw.append(raw)
         nc.vector.memset(warm[:], 0.0)
-        nc.vector.memset(planes[:].rearrange("p g s n -> p (g s n)").bitcast(I32), 0)
+        for planes, engine in ((k_planes, nc.vector), (c_planes, nc.gpsimd)):
+            engine.memset(planes[:].rearrange("p g n -> p (g n)").bitcast(I32), 0)
 
         nc.scalar.activation(warm_out[:], warm[:], ACT.Sigmoid)
 
-        nc.vector.tensor_copy(s_got[:, 0, :], ks_win[:].indirect(offsets[:]))
-        nc.vector.tensor_copy(s_got[:, 1, :], cs_win[:].indirect(offsets[:]))
+        nc.vector.tensor_copy(ks_got[:], ks_win[:].indirect(offsets[:]))
         for quad in range(4):
-            nc.scalar.dma_start(
-                out=planes[32 * quad : 32 * quad + 4].rearrange("p g s n -> p g (s n)").bitcast(I32),
-                in_=s_got[96 + 8 * quad : 96 + 8 * quad + 8].rearrange("p s n -> p (s n)").bitcast(I32),
-            )
+            place(nc.sync if quad < 2 else nc.scalar, k_planes, ks_got, 96, quad)
+        cw_win = pool.tile([P, T], I32, name="cw_win", tag="ks_then_cw", align_bytes=64)
+        load_words(cw_win, c_words)
+        nc.vector.tensor_copy(cs_got[:], cs_win[:].indirect(offsets[:]))
+        for quad in range(4):
+            place(nc.sync, c_planes, cs_got, 32, quad)
 
         kw_got = pool.tile([P, N], U32, name="kw_got", align_bytes=64)
         kw = pool.tile([P, PASSES, N], U16, name="kw", align_bytes=64)
@@ -75,45 +87,56 @@ def tile_attend_twokey_topk_kernel(tc, qT, k_words, k_scales, c_words, c_scales,
         q_codes = pool.tile([P, PASSES * NQ], U32, name="q_codes", align_bytes=64)
         q_scales = pool.tile([P, PASSES * NQ], U8, name="q_scales", align_bytes=64)
         for g in range(PASSES):
-            nc.scalar.activation(q_bf[:, g], q_raw[:, g].rearrange("p j w -> p w j"), ACT.Copy)
+            nc.scalar.activation(q_bf[:, g], q_raw[g][:].rearrange("p j w -> p w j"), ACT.Copy)
         nc.vector.quantize_mx(
             out=q_codes[:].bitcast(FP8X4), scales=q_scales[:], in_=q_bf[:].rearrange("p g w j -> p (g w j)")
         )
 
-        def product(acc, words, table, cols, wcols):
+        def product(acc, words, planes, cols, wcols):
             for g in range(PASSES):
                 nc.tensor.matmul_mx(
                     out=acc,
                     lhsT=q_codes[:, g * NQ : (g + 1) * NQ].bitcast(FP8X4),
                     lhsT_scale=q_scales[:, g * NQ : (g + 1) * NQ],
                     rhs=words[:, g, wcols].bitcast(FP4X4),
-                    rhs_scale=planes[:, g, table, cols],
+                    rhs_scale=planes[:, g, cols],
                     start=(g == 0),
                     stop=(g == PASSES - 1),
                 )
 
         a_ps = psum.tile([P, N], F32, name="a_ps")
-        product(a_ps[:], kw, 0, slice(0, N), slice(0, N))
+        product(a_ps[:], kw, k_planes, slice(0, N), slice(0, N))
+        keep_ps = psum.tile([P, N], F32, name="keep_ps")
+        nc.tensor.matmul_mx(
+            out=keep_ps[:],
+            lhsT=q_codes[:, NQ : 2 * NQ].bitcast(FP8X4),
+            lhsT_scale=q_scales[:, NQ : 2 * NQ],
+            rhs=kw[:, 1, :].bitcast(FP4X4),
+            rhs_scale=k_planes[:, 1, :],
+            start=True,
+            stop=True,
+        )
         gate = pool.tile([P, N], F32, name="gate")
-        nc.scalar.activation(gate[:], a_ps[:], ACT.Sigmoid)
+        for h in range(2):
+            nc.scalar.activation(gate[:, h * HALF : (h + 1) * HALF], a_ps[:, h * HALF : (h + 1) * HALF], ACT.Sigmoid)
 
-        z_ps = []
+        cw_got = []
         for h in range(2):
             got = pool.tile([P, HALF], U32, name="cw_got%d" % h, align_bytes=64)
             nc.vector.tensor_copy(got[:], cw_win[:].bitcast(U32).indirect(offsets[:, h * 16 : (h + 1) * 16]))
-            z = psum.tile([P, N], F32, name="z_ps%d" % h)
-            for s in range(2):
-                c0 = h * HALF + s * P
-                if h == 1 or s == 0:
-                    width = P if h == 1 else HALF
-                    cw = pool.tile([P, PASSES, width], U16, name="cw%d%d" % (h, s), align_bytes=64)
-                    src = got[:, s * P : s * P + width].bitcast(U16)
-                    nc.vector.tensor_copy(cw[:], src.rearrange("p (n g) -> p g n", g=PASSES))
-                w0 = 0 if h == 1 else s * P
-                product(z[:, s * P : (s + 1) * P], cw, 1, slice(c0, c0 + P), slice(w0, w0 + P))
-            z_ps.append(z)
+            cw_got.append(got)
 
-        for h in range(2):
-            y = pool.tile([P, HALF], F32, name="y%d" % h)
-            nc.vector.tensor_tensor(y[:], z_ps[h][:, 0:HALF], gate[:, h * HALF : (h + 1) * HALF], ALU.mult)
-            nc.sync.dma_start(out=out[0][:, h * HALF : (h + 1) * HALF], in_=y[:])
+        z_ps = [psum.tile([P, N], F32, name="z_ps%d" % i) for i in range(3)]
+        z_of = [z_ps[0][:, 0:P], z_ps[0][:, P:HALF], z_ps[1][:, 0:P], z_ps[2][:, 0:P]]
+        for s in range(4):
+            cw = pool.tile([P, PASSES, P], U16, name="cw%d" % s, align_bytes=64)
+            src = cw_got[s // 2][:, (s % 2) * P : (s % 2 + 1) * P].bitcast(U16)
+            nc.vector.tensor_copy(cw[:], src.rearrange("p (n g) -> p g n", g=PASSES))
+            product(z_of[s], cw, c_planes, slice(s * P, (s + 1) * P), slice(0, P))
+
+        y = [pool.tile([P, HALF], F32, name="y%d" % h) for h in range(2)]
+        nc.vector.tensor_tensor(y[0][:], z_ps[0][:, 0:HALF], gate[:, 0:HALF], ALU.mult)
+        nc.sync.dma_start(out=out[0][:, 0:HALF], in_=y[0][:])
+        for s in range(2, 4):
+            nc.vector.tensor_tensor(y[1][:, (s - 2) * P : (s - 1) * P], z_of[s], gate[:, s * P : (s + 1) * P], ALU.mult)
+        nc.sync.dma_start(out=out[0][:, HALF:N], in_=y[1][:])

@@ -20,6 +20,7 @@ P = 128
 PACK = 4
 PASSES = 2
 HALF = N // 2
+EARLY = T // 4
 
 
 def tile_attend_twokey_topk_kernel(tc, qT, k_words, k_scales, c_words, c_scales, offs, out):
@@ -58,11 +59,11 @@ def tile_attend_twokey_topk_kernel(tc, qT, k_words, k_scales, c_words, c_scales,
         load_scales(ks_win, k_scales, 96, [(0, 96)], nc.vector)
         load_scales(cs_win, c_scales, 32, [(0, 32), (64, P)], nc.gpsimd)
         load_words(kw_win, k_words)
-        q_raw = []
-        for g in range(PASSES):
-            raw = pool.tile([P, PACK, NQ], F32, name="q_raw%d" % g)
-            nc.sync.dma_start(out=raw[:], in_=qT[0].rearrange("(g p j) w -> g p j w", g=PASSES, j=PACK)[g])
-            q_raw.append(raw)
+        q_raw = pool.tile([P, PASSES, PACK, NQ], F32, name="q_raw")
+        nc.sync.dma_start(out=q_raw[:], in_=qT[0].rearrange("(g p j) w -> p g j w", g=PASSES, j=PACK))
+        c_rows = c_words[0].rearrange("p t b -> p (t b)").bitcast(I32)
+        cw_early = pool.tile([P, EARLY], I32, name="cw_early", align_bytes=64)
+        nc.sync.dma_start(out=cw_early[:], in_=c_rows[:, 0:EARLY])
         nc.vector.memset(warm[:], 0.0)
         for planes, engine in ((k_planes, nc.vector), (c_planes, nc.gpsimd)):
             engine.memset(planes[:].rearrange("p g n -> p (g n)").bitcast(I32), 0)
@@ -73,7 +74,7 @@ def tile_attend_twokey_topk_kernel(tc, qT, k_words, k_scales, c_words, c_scales,
         for quad in range(4):
             place(nc.sync if quad < 2 else nc.scalar, k_planes, ks_got, 96, quad)
         cw_win = pool.tile([P, T], I32, name="cw_win", tag="ks_then_cw", align_bytes=64)
-        load_words(cw_win, c_words)
+        nc.sync.dma_start(out=cw_win[:, EARLY:T], in_=c_rows[:, EARLY:T])
         nc.vector.tensor_copy(cs_got[:], cs_win[:].indirect(offsets[:]))
         for quad in range(4):
             place(nc.sync, c_planes, cs_got, 32, quad)
@@ -87,25 +88,25 @@ def tile_attend_twokey_topk_kernel(tc, qT, k_words, k_scales, c_words, c_scales,
         q_codes = pool.tile([P, PASSES * NQ], U32, name="q_codes", align_bytes=64)
         q_scales = pool.tile([P, PASSES * NQ], U8, name="q_scales", align_bytes=64)
         for g in range(PASSES):
-            nc.scalar.activation(q_bf[:, g], q_raw[g][:].rearrange("p j w -> p w j"), ACT.Copy)
+            nc.scalar.activation(q_bf[:, g], q_raw[:, g].rearrange("p j w -> p w j"), ACT.Copy)
         nc.vector.quantize_mx(
             out=q_codes[:].bitcast(FP8X4), scales=q_scales[:], in_=q_bf[:].rearrange("p g w j -> p (g w j)")
         )
 
-        def product(acc, words, planes, cols, wcols):
-            for g in range(PASSES):
+        def product(acc, words, planes, cols, wcols, order):
+            for g in order:
                 nc.tensor.matmul_mx(
                     out=acc,
                     lhsT=q_codes[:, g * NQ : (g + 1) * NQ].bitcast(FP8X4),
                     lhsT_scale=q_scales[:, g * NQ : (g + 1) * NQ],
                     rhs=words[:, g, wcols].bitcast(FP4X4),
                     rhs_scale=planes[:, g, cols],
-                    start=(g == 0),
-                    stop=(g == PASSES - 1),
+                    start=(g == order[0]),
+                    stop=(g == order[-1]),
                 )
 
         a_ps = psum.tile([P, N], F32, name="a_ps")
-        product(a_ps[:], kw, k_planes, slice(0, N), slice(0, N))
+        product(a_ps[:], kw, k_planes, slice(0, N), slice(0, N), (0, 1))
         keep_ps = psum.tile([P, N], F32, name="keep_ps")
         nc.tensor.matmul_mx(
             out=keep_ps[:],
@@ -120,23 +121,23 @@ def tile_attend_twokey_topk_kernel(tc, qT, k_words, k_scales, c_words, c_scales,
         for h in range(2):
             nc.scalar.activation(gate[:, h * HALF : (h + 1) * HALF], a_ps[:, h * HALF : (h + 1) * HALF], ACT.Sigmoid)
 
+        nc.vector.tensor_copy(cw_win[:, 0:EARLY], cw_early[:])
         cw_got = []
         for h in range(2):
             got = pool.tile([P, HALF], U32, name="cw_got%d" % h, align_bytes=64)
             nc.vector.tensor_copy(got[:], cw_win[:].bitcast(U32).indirect(offsets[:, h * 16 : (h + 1) * 16]))
             cw_got.append(got)
 
-        z_ps = [psum.tile([P, N], F32, name="z_ps%d" % i) for i in range(3)]
-        z_of = [z_ps[0][:, 0:P], z_ps[0][:, P:HALF], z_ps[1][:, 0:P], z_ps[2][:, 0:P]]
+        z_ps = [psum.tile([P, P], F32, name="z_ps%d" % s) for s in range(4)]
         for s in range(4):
             cw = pool.tile([P, PASSES, P], U16, name="cw%d" % s, align_bytes=64)
             src = cw_got[s // 2][:, (s % 2) * P : (s % 2 + 1) * P].bitcast(U16)
             nc.vector.tensor_copy(cw[:], src.rearrange("p (n g) -> p g n", g=PASSES))
-            product(z_of[s], cw, c_planes, slice(s * P, (s + 1) * P), slice(0, P))
+            product(z_ps[s][:], cw, c_planes, slice(s * P, (s + 1) * P), slice(0, P), (1, 0) if s % 2 == 0 else (0, 1))
 
-        y = [pool.tile([P, HALF], F32, name="y%d" % h) for h in range(2)]
-        nc.vector.tensor_tensor(y[0][:], z_ps[0][:, 0:HALF], gate[:, 0:HALF], ALU.mult)
-        nc.sync.dma_start(out=out[0][:, 0:HALF], in_=y[0][:])
-        for s in range(2, 4):
-            nc.vector.tensor_tensor(y[1][:, (s - 2) * P : (s - 1) * P], z_of[s], gate[:, s * P : (s + 1) * P], ALU.mult)
-        nc.sync.dma_start(out=out[0][:, HALF:N], in_=y[1][:])
+        for h in range(2):
+            y = pool.tile([P, HALF], F32, name="y%d" % h)
+            for i in range(2):
+                s = 2 * h + i
+                nc.vector.tensor_tensor(y[:, i * P : (i + 1) * P], z_ps[s][:], gate[:, s * P : (s + 1) * P], ALU.mult)
+            nc.sync.dma_start(out=out[0][:, h * HALF : (h + 1) * HALF], in_=y[:])

@@ -20,7 +20,6 @@ P = 128
 PACK = 4
 PASSES = 2
 HALF = N // 2
-EARLY = T // 4
 
 
 def tile_attend_twokey_topk_kernel(tc, qT, k_words, k_scales, c_words, c_scales, offs, out):
@@ -30,8 +29,9 @@ def tile_attend_twokey_topk_kernel(tc, qT, k_words, k_scales, c_words, c_scales,
         psum = ctx.enter_context(tc.psum_pool(name="psum", bufs=1))
 
         offsets = pool.tile([P, N // 16], U16, name="offsets")
-        ks_win = pool.tile([P, T], U8, name="ks_win", tag="ks_then_cw", align_bytes=64)
+        ks_win = pool.tile([P, T], U8, name="ks_win", align_bytes=64)
         cs_win = pool.tile([P, T], U8, name="cs_win", align_bytes=64)
+        cw_win = pool.tile([P, T], I32, name="cw_win", align_bytes=64)
         kw_win = pool.tile([P, T], I32, name="kw_win", align_bytes=64)
         ks_got = pool.tile([P, N], U8, name="ks_got", align_bytes=64)
         cs_got = pool.tile([P, N], U8, name="cs_got", align_bytes=64)
@@ -57,24 +57,20 @@ def tile_attend_twokey_topk_kernel(tc, qT, k_words, k_scales, c_words, c_scales,
 
         nc.sync.dma_start(offsets[:], offs)
         load_scales(ks_win, k_scales, 96, [(0, 96)], nc.vector)
-        load_scales(cs_win, c_scales, 32, [(0, 32), (64, P)], nc.gpsimd)
+        load_scales(cs_win, c_scales, 32, [(0, 32), (64, P)], nc.vector)
         load_words(kw_win, k_words)
         q_raw = pool.tile([P, PASSES, PACK, NQ], F32, name="q_raw")
         nc.sync.dma_start(out=q_raw[:], in_=qT[0].rearrange("(g p j) w -> p g j w", g=PASSES, j=PACK))
-        c_rows = c_words[0].rearrange("p t b -> p (t b)").bitcast(I32)
-        cw_early = pool.tile([P, EARLY], I32, name="cw_early", align_bytes=64)
-        nc.sync.dma_start(out=cw_early[:], in_=c_rows[:, 0:EARLY])
+        load_words(cw_win, c_words)
         nc.vector.memset(warm[:], 0.0)
-        for planes, engine in ((k_planes, nc.vector), (c_planes, nc.gpsimd)):
+        for planes, engine in ((k_planes, nc.vector), (c_planes, nc.vector)):
             engine.memset(planes[:].rearrange("p g n -> p (g n)").bitcast(I32), 0)
 
         nc.scalar.activation(warm_out[:], warm[:], ACT.Sigmoid)
 
         nc.vector.tensor_copy(ks_got[:], ks_win[:].indirect(offsets[:]))
         for quad in range(4):
-            place(nc.sync if quad < 2 else nc.scalar, k_planes, ks_got, 96, quad)
-        cw_win = pool.tile([P, T], I32, name="cw_win", tag="ks_then_cw", align_bytes=64)
-        nc.sync.dma_start(out=cw_win[:, EARLY:T], in_=c_rows[:, EARLY:T])
+            place(nc.scalar, k_planes, ks_got, 96, quad)
         nc.vector.tensor_copy(cs_got[:], cs_win[:].indirect(offsets[:]))
         for quad in range(4):
             place(nc.sync, c_planes, cs_got, 32, quad)
@@ -121,7 +117,6 @@ def tile_attend_twokey_topk_kernel(tc, qT, k_words, k_scales, c_words, c_scales,
         for h in range(2):
             nc.scalar.activation(gate[:, h * HALF : (h + 1) * HALF], a_ps[:, h * HALF : (h + 1) * HALF], ACT.Sigmoid)
 
-        nc.vector.tensor_copy(cw_win[:, 0:EARLY], cw_early[:])
         cw_got = []
         for h in range(2):
             got = pool.tile([P, HALF], U32, name="cw_got%d" % h, align_bytes=64)

@@ -103,16 +103,6 @@ def tile_attend_twokey_topk_kernel(tc, qT, k_words, k_scales, c_words, c_scales,
 
         a_ps = psum.tile([P, N], F32, name="a_ps")
         product(a_ps[:], kw, k_planes, slice(0, N), slice(0, N), (0, 1))
-        keep_ps = psum.tile([P, N], F32, name="keep_ps")
-        nc.tensor.matmul_mx(
-            out=keep_ps[:],
-            lhsT=q_codes[:, NQ : 2 * NQ].bitcast(FP8X4),
-            lhsT_scale=q_scales[:, NQ : 2 * NQ],
-            rhs=kw[:, 1, :].bitcast(FP4X4),
-            rhs_scale=k_planes[:, 1, :],
-            start=True,
-            stop=True,
-        )
         gate = pool.tile([P, N], F32, name="gate")
         for h in range(2):
             nc.scalar.activation(gate[:, h * HALF : (h + 1) * HALF], a_ps[:, h * HALF : (h + 1) * HALF], ACT.Sigmoid)

@@ -101,6 +101,16 @@ def tile_attend_twokey_topk_kernel(tc, qT, k_words, k_scales, c_words, c_scales,
                     stop=(g == order[-1]),
                 )
 
+        keep_ps = psum.tile([P, N], F32, name="keep_ps")
+        nc.tensor.matmul_mx(
+            out=keep_ps[:],
+            lhsT=q_codes[:, 0:NQ].bitcast(FP8X4),
+            lhsT_scale=q_scales[:, 0:NQ],
+            rhs=kw[:, 0, :].bitcast(FP4X4),
+            rhs_scale=ks_got[:],
+            start=True,
+            stop=True,
+        )
         a_ps = psum.tile([P, N], F32, name="a_ps")
         product(a_ps[:], kw, k_planes, slice(0, N), slice(0, N), (0, 1))
         gate = pool.tile([P, N], F32, name="gate")

@@ -80,21 +80,24 @@ def tile_attend_twokey_topk_kernel(tc, qT, k_words, k_scales, c_words, c_scales,
         nc.vector.tensor_copy(kw_got[:], kw_win[:].bitcast(U32).indirect(offsets[:]))
         nc.vector.tensor_copy(kw[:], kw_got[:].bitcast(U16).rearrange("p (n g) -> p g n", g=PASSES))
 
-        q_bf = pool.tile([P, PASSES, NQ, PACK], BF16, name="q_bf", align_bytes=64)
-        q_codes = pool.tile([P, PASSES * NQ], U32, name="q_codes", align_bytes=64)
-        q_scales = pool.tile([P, PASSES * NQ], U8, name="q_scales", align_bytes=64)
+        q_codes, q_scales = [], []
         for g in range(PASSES):
-            nc.scalar.activation(q_bf[:, g], q_raw[:, g].rearrange("p j w -> p w j"), ACT.Copy)
-        nc.vector.quantize_mx(
-            out=q_codes[:].bitcast(FP8X4), scales=q_scales[:], in_=q_bf[:].rearrange("p g w j -> p (g w j)")
-        )
+            q_bf = pool.tile([P, NQ, PACK], BF16, name="q_bf%d" % g, align_bytes=64)
+            codes = pool.tile([P, NQ], U32, name="q_codes%d" % g, align_bytes=64)
+            scales = pool.tile([P, NQ], U8, name="q_scales%d" % g, align_bytes=64)
+            nc.scalar.activation(q_bf[:], q_raw[:, g].rearrange("p j w -> p w j"), ACT.Copy)
+            nc.vector.quantize_mx(
+                out=codes[:].bitcast(FP8X4), scales=scales[:], in_=q_bf[:].rearrange("p w j -> p (w j)")
+            )
+            q_codes.append(codes)
+            q_scales.append(scales)
 
         def product(acc, words, planes, cols, wcols, order):
             for g in order:
                 nc.tensor.matmul_mx(
                     out=acc,
-                    lhsT=q_codes[:, g * NQ : (g + 1) * NQ].bitcast(FP8X4),
-                    lhsT_scale=q_scales[:, g * NQ : (g + 1) * NQ],
+                    lhsT=q_codes[g][:].bitcast(FP8X4),
+                    lhsT_scale=q_scales[g][:],
                     rhs=words[:, g, wcols].bitcast(FP4X4),
                     rhs_scale=planes[:, g, cols],
                     start=(g == order[0]),
@@ -104,8 +107,8 @@ def tile_attend_twokey_topk_kernel(tc, qT, k_words, k_scales, c_words, c_scales,
         keep_ps = psum.tile([P, N], F32, name="keep_ps")
         nc.tensor.matmul_mx(
             out=keep_ps[:],
-            lhsT=q_codes[:, 0:NQ].bitcast(FP8X4),
-            lhsT_scale=q_scales[:, 0:NQ],
+            lhsT=q_codes[0][:].bitcast(FP8X4),
+            lhsT_scale=q_scales[0][:],
             rhs=kw[:, 0, :].bitcast(FP4X4),
             rhs_scale=ks_got[:],
             start=True,

@@ -104,16 +104,6 @@ def tile_attend_twokey_topk_kernel(tc, qT, k_words, k_scales, c_words, c_scales,
                     stop=(g == order[-1]),
                 )
 
-        keep_ps = psum.tile([P, N], F32, name="keep_ps")
-        nc.tensor.matmul_mx(
-            out=keep_ps[:],
-            lhsT=q_codes[0][:].bitcast(FP8X4),
-            lhsT_scale=q_scales[0][:],
-            rhs=kw[:, 0, :].bitcast(FP4X4),
-            rhs_scale=ks_got[:],
-            start=True,
-            stop=True,
-        )
         a_ps = psum.tile([P, N], F32, name="a_ps")
         product(a_ps[:], kw, k_planes, slice(0, N), slice(0, N), (0, 1))
         gate = pool.tile([P, N], F32, name="gate")

@@ -29,14 +29,12 @@ def tile_attend_twokey_topk_kernel(tc, qT, k_words, k_scales, c_words, c_scales,
         psum = ctx.enter_context(tc.psum_pool(name="psum", bufs=1))
 
         offsets = pool.tile([P, N // 16], U16, name="offsets")
-        ks_win = pool.tile([P, T], U8, name="ks_win", align_bytes=64)
-        cs_win = pool.tile([P, T], U8, name="cs_win", align_bytes=64)
+        ks_win = pool.tile([P, T], U8, name="ks_win", tag="k_bytes", align_bytes=64)
+        cs_win = pool.tile([P, T], U8, name="cs_win", tag="c_bytes", align_bytes=64)
         cw_win = pool.tile([P, T], I32, name="cw_win", align_bytes=64)
         kw_win = pool.tile([P, T], I32, name="kw_win", align_bytes=64)
         ks_got = pool.tile([P, N], U8, name="ks_got", align_bytes=64)
         cs_got = pool.tile([P, N], U8, name="cs_got", align_bytes=64)
-        k_planes = pool.tile([P, PASSES, N], U8, name="k_planes", align_bytes=64)
-        c_planes = pool.tile([P, PASSES, N], U8, name="c_planes", align_bytes=64)
         warm = pool.tile([P, 8], F32, name="warm")
         warm_out = pool.tile([P, 8], F32, name="warm_out")
 
@@ -55,23 +53,23 @@ def tile_attend_twokey_topk_kernel(tc, qT, k_words, k_scales, c_words, c_scales,
         def load_words(win, words):
             nc.sync.dma_start(out=win[:], in_=words[0].rearrange("p t b -> p (t b)").bitcast(I32))
 
-        nc.sync.dma_start(offsets[:], offs)
         load_scales(ks_win, k_scales, 96, [(0, 96)], nc.vector)
+        nc.sync.dma_start(offsets[:], offs)
         load_scales(cs_win, c_scales, 32, [(0, 32), (64, P)], nc.vector)
         load_words(kw_win, k_words)
         q_raw = pool.tile([P, PASSES, PACK, NQ], F32, name="q_raw")
         nc.sync.dma_start(out=q_raw[:], in_=qT[0].rearrange("(g p j) w -> p g j w", g=PASSES, j=PACK))
         load_words(cw_win, c_words)
         nc.vector.memset(warm[:], 0.0)
-        for planes, engine in ((k_planes, nc.vector), (c_planes, nc.vector)):
-            engine.memset(planes[:].rearrange("p g n -> p (g n)").bitcast(I32), 0)
 
         nc.scalar.activation(warm_out[:], warm[:], ACT.Sigmoid)
 
         nc.vector.tensor_copy(ks_got[:], ks_win[:].indirect(offsets[:]))
+        k_planes = pool.tile([P, PASSES, N], U8, name="k_planes", tag="k_bytes", align_bytes=64)
         for quad in range(4):
             place(nc.scalar, k_planes, ks_got, 96, quad)
         nc.vector.tensor_copy(cs_got[:], cs_win[:].indirect(offsets[:]))
+        c_planes = pool.tile([P, PASSES, N], U8, name="c_planes", tag="c_bytes", align_bytes=64)
         for quad in range(4):
             place(nc.sync, c_planes, cs_got, 32, quad)
 

@@ -102,6 +102,16 @@ def tile_attend_twokey_topk_kernel(tc, qT, k_words, k_scales, c_words, c_scales,
                     stop=(g == order[-1]),
                 )
 
+        warm_ps = psum.tile([P, N], F32, name="warm_ps")
+        nc.tensor.matmul_mx(
+            out=warm_ps[:],
+            lhsT=q_codes[0][:].bitcast(FP8X4),
+            lhsT_scale=q_scales[0][:],
+            rhs=kw[:, 0].bitcast(FP4X4),
+            rhs_scale=ks_got[:],
+            start=True,
+            stop=True,
+        )
         a_ps = psum.tile([P, N], F32, name="a_ps")
         product(a_ps[:], kw, k_planes, slice(0, N), slice(0, N), (0, 1))
         gate = pool.tile([P, N], F32, name="gate")
@@ -118,7 +128,12 @@ def tile_attend_twokey_topk_kernel(tc, qT, k_words, k_scales, c_words, c_scales,
         for s in range(4):
             cw = pool.tile([P, PASSES, P], U16, name="cw%d" % s, align_bytes=64)
             src = cw_got[s // 2][:, (s % 2) * P : (s % 2 + 1) * P].bitcast(U16)
-            nc.vector.tensor_copy(cw[:], src.rearrange("p (n g) -> p g n", g=PASSES))
+            halves = src.rearrange("p (n g) -> p g n", g=PASSES)
+            if s == 0:
+                for g in (1, 0):
+                    nc.vector.tensor_copy(cw[:, g], halves[:, g])
+            else:
+                nc.vector.tensor_copy(cw[:], halves)
             product(z_ps[s][:], cw, c_planes, slice(s * P, (s + 1) * P), slice(0, P), (1, 0) if s % 2 == 0 else (0, 1))
 
         for h in range(2):

@@ -35,8 +35,6 @@ def tile_attend_twokey_topk_kernel(tc, qT, k_words, k_scales, c_words, c_scales,
         kw_win = pool.tile([P, T], I32, name="kw_win", align_bytes=64)
         ks_got = pool.tile([P, N], U8, name="ks_got", align_bytes=64)
         cs_got = pool.tile([P, N], U8, name="cs_got", align_bytes=64)
-        warm = pool.tile([P, 8], F32, name="warm")
-        warm_out = pool.tile([P, 8], F32, name="warm_out")
 
         def load_scales(win, scales, first, blanks, engine):
             rows = scales.rearrange("o f t -> f o t")
@@ -60,9 +58,6 @@ def tile_attend_twokey_topk_kernel(tc, qT, k_words, k_scales, c_words, c_scales,
         q_raw = pool.tile([P, PASSES, PACK, NQ], F32, name="q_raw")
         nc.sync.dma_start(out=q_raw[:], in_=qT[0].rearrange("(g p j) w -> p g j w", g=PASSES, j=PACK))
         load_words(cw_win, c_words)
-        nc.vector.memset(warm[:], 0.0)
-
-        nc.scalar.activation(warm_out[:], warm[:], ACT.Sigmoid)
 
         nc.vector.tensor_copy(ks_got[:], ks_win[:].indirect(offsets[:]))
         k_planes = pool.tile([P, PASSES, N], U8, name="k_planes", tag="k_bytes", align_bytes=64)
@@ -83,7 +78,7 @@ def tile_attend_twokey_topk_kernel(tc, qT, k_words, k_scales, c_words, c_scales,
             q_bf = pool.tile([P, NQ, PACK], BF16, name="q_bf%d" % g, align_bytes=64)
             codes = pool.tile([P, NQ], U32, name="q_codes%d" % g, align_bytes=64)
             scales = pool.tile([P, NQ], U8, name="q_scales%d" % g, align_bytes=64)
-            nc.scalar.activation(q_bf[:], q_raw[:, g].rearrange("p j w -> p w j"), ACT.Copy)
+            nc.vector.tensor_copy(q_bf[:], q_raw[:, g].rearrange("p j w -> p w j"))
             nc.vector.quantize_mx(
                 out=codes[:].bitcast(FP8X4), scales=scales[:], in_=q_bf[:].rearrange("p w j -> p (w j)")
             )
@@ -129,8 +124,8 @@ def tile_attend_twokey_topk_kernel(tc, qT, k_words, k_scales, c_words, c_scales,
             cw = pool.tile([P, PASSES, P], U16, name="cw%d" % s, align_bytes=64)
             src = cw_got[s // 2][:, (s % 2) * P : (s % 2 + 1) * P].bitcast(U16)
             halves = src.rearrange("p (n g) -> p g n", g=PASSES)
-            if s == 0:
-                for g in (1, 0):
+            if s in (0, 3):
+                for g in (1, 0) if s == 0 else (0, 1):
                     nc.vector.tensor_copy(cw[:, g], halves[:, g])
             else:
                 nc.vector.tensor_copy(cw[:], halves)

@@ -54,9 +54,9 @@ def tile_attend_twokey_topk_kernel(tc, qT, k_words, k_scales, c_words, c_scales,
         load_scales(ks_win, k_scales, 96, [(0, 96)], nc.vector)
         nc.sync.dma_start(offsets[:], offs)
         load_scales(cs_win, c_scales, 32, [(0, 32), (64, P)], nc.vector)
-        load_words(kw_win, k_words)
         q_raw = pool.tile([P, PASSES, PACK, NQ], F32, name="q_raw")
         nc.sync.dma_start(out=q_raw[:], in_=qT[0].rearrange("(g p j) w -> p g j w", g=PASSES, j=PACK))
+        load_words(kw_win, k_words)
         load_words(cw_win, c_words)
 
         nc.vector.tensor_copy(ks_got[:], ks_win[:].indirect(offsets[:]))
@@ -71,7 +71,8 @@ def tile_attend_twokey_topk_kernel(tc, qT, k_words, k_scales, c_words, c_scales,
         kw_got = pool.tile([P, N], U32, name="kw_got", align_bytes=64)
         kw = pool.tile([P, PASSES, N], U16, name="kw", align_bytes=64)
         nc.vector.tensor_copy(kw_got[:], kw_win[:].bitcast(U32).indirect(offsets[:]))
-        nc.vector.tensor_copy(kw[:], kw_got[:].bitcast(U16).rearrange("p (n g) -> p g n", g=PASSES))
+        for g in range(PASSES):
+            nc.vector.tensor_copy(kw[:, g], kw_got[:].bitcast(U16).rearrange("p (n g) -> p g n", g=PASSES)[:, g])
 
         q_codes, q_scales = [], []
         for g in range(PASSES):

@@ -62,7 +62,7 @@ def tile_attend_twokey_topk_kernel(tc, qT, k_words, k_scales, c_words, c_scales,
         nc.vector.tensor_copy(ks_got[:], ks_win[:].indirect(offsets[:]))
         k_planes = pool.tile([P, PASSES, N], U8, name="k_planes", tag="k_bytes", align_bytes=64)
         for quad in range(4):
-            place(nc.scalar, k_planes, ks_got, 96, quad)
+            place(nc.sync, k_planes, ks_got, 96, quad)
         nc.vector.tensor_copy(cs_got[:], cs_win[:].indirect(offsets[:]))
         c_planes = pool.tile([P, PASSES, N], U8, name="c_planes", tag="c_bytes", align_bytes=64)
         for quad in range(4):
@@ -79,7 +79,7 @@ def tile_attend_twokey_topk_kernel(tc, qT, k_words, k_scales, c_words, c_scales,
             q_bf = pool.tile([P, NQ, PACK], BF16, name="q_bf%d" % g, align_bytes=64)
             codes = pool.tile([P, NQ], U32, name="q_codes%d" % g, align_bytes=64)
             scales = pool.tile([P, NQ], U8, name="q_scales%d" % g, align_bytes=64)
-            nc.vector.tensor_copy(q_bf[:], q_raw[:, g].rearrange("p j w -> p w j"))
+            nc.scalar.activation(q_bf[:], q_raw[:, g].rearrange("p j w -> p w j"), ACT.Copy)
             nc.vector.quantize_mx(
                 out=codes[:].bitcast(FP8X4), scales=scales[:], in_=q_bf[:].rearrange("p w j -> p (w j)")
             )
@@ -108,11 +108,12 @@ def tile_attend_twokey_topk_kernel(tc, qT, k_words, k_scales, c_words, c_scales,
             start=True,
             stop=True,
         )
-        a_ps = psum.tile([P, N], F32, name="a_ps")
-        product(a_ps[:], kw, k_planes, slice(0, N), slice(0, N), (0, 1))
         gate = pool.tile([P, N], F32, name="gate")
         for h in range(2):
-            nc.scalar.activation(gate[:, h * HALF : (h + 1) * HALF], a_ps[:, h * HALF : (h + 1) * HALF], ACT.Sigmoid)
+            cols = slice(h * HALF, (h + 1) * HALF)
+            a_ps = psum.tile([P, HALF], F32, name="a_ps%d" % h)
+            product(a_ps[:], kw, k_planes, cols, cols, (0, 1) if h == 0 else (1, 0))
+            nc.scalar.activation(gate[:, cols], a_ps[:], ACT.Sigmoid)
 
         cw_got = []
         for h in range(2):
@@ -126,11 +127,11 @@ def tile_attend_twokey_topk_kernel(tc, qT, k_words, k_scales, c_words, c_scales,
             src = cw_got[s // 2][:, (s % 2) * P : (s % 2 + 1) * P].bitcast(U16)
             halves = src.rearrange("p (n g) -> p g n", g=PASSES)
             if s in (0, 3):
-                for g in (1, 0) if s == 0 else (0, 1):
+                for g in (0, 1) if s == 0 else (1, 0):
                     nc.vector.tensor_copy(cw[:, g], halves[:, g])
             else:
                 nc.vector.tensor_copy(cw[:], halves)
-            product(z_ps[s][:], cw, c_planes, slice(s * P, (s + 1) * P), slice(0, P), (1, 0) if s % 2 == 0 else (0, 1))
+            product(z_ps[s][:], cw, c_planes, slice(s * P, (s + 1) * P), slice(0, P), (0, 1) if s % 2 == 0 else (1, 0))
 
         for h in range(2):
             y = pool.tile([P, HALF], F32, name="y%d" % h)

@@ -98,16 +98,6 @@ def tile_attend_twokey_topk_kernel(tc, qT, k_words, k_scales, c_words, c_scales,
                     stop=(g == order[-1]),
                 )
 
-        warm_ps = psum.tile([P, N], F32, name="warm_ps")
-        nc.tensor.matmul_mx(
-            out=warm_ps[:],
-            lhsT=q_codes[0][:].bitcast(FP8X4),
-            lhsT_scale=q_scales[0][:],
-            rhs=kw[:, 0].bitcast(FP4X4),
-            rhs_scale=ks_got[:],
-            start=True,
-            stop=True,
-        )
         gate = pool.tile([P, N], F32, name="gate")
         for h in range(2):
             cols = slice(h * HALF, (h + 1) * HALF)

@@ -42,31 +42,34 @@ def tile_attend_twokey_topk_kernel(tc, qT, k_words, k_scales, c_words, c_scales,
             for lo, hi in blanks:
                 engine.memset(win[lo:hi, :].bitcast(I32), 0)
 
-        def place(queue, planes, got, first, quad):
+        def place(queue, planes, got, first, quad, step):
             queue.dma_start(
                 out=planes[32 * quad : 32 * quad + 4].bitcast(I32),
-                in_=got[first + 8 * quad : first + 8 * quad + 8].bitcast(I32),
+                in_=got[first + 8 * step * quad : first + 8 * step * (quad + 1) : step].bitcast(I32),
             )
 
         def load_words(win, words):
             nc.sync.dma_start(out=win[:], in_=words[0].rearrange("p t b -> p (t b)").bitcast(I32))
 
+        nc.vector.memset(cs_win[:].bitcast(I32), 0)
         load_scales(ks_win, k_scales, 96, [(0, 96)], nc.vector)
         nc.sync.dma_start(offsets[:], offs)
-        load_scales(cs_win, c_scales, 32, [(0, 32), (64, P)], nc.vector)
         q_raw = pool.tile([P, PASSES, PACK, NQ], F32, name="q_raw")
         nc.sync.dma_start(out=q_raw[:], in_=qT[0].rearrange("(g p j) w -> p g j w", g=PASSES, j=PACK))
+        nc.sync.dma_start(
+            out=cs_win[32:96:2, :].bitcast(I32), in_=c_scales.rearrange("o f t -> f o t").bitcast(I32)
+        )
         load_words(kw_win, k_words)
         load_words(cw_win, c_words)
 
         nc.vector.tensor_copy(ks_got[:], ks_win[:].indirect(offsets[:]))
         k_planes = pool.tile([P, PASSES, N], U8, name="k_planes", tag="k_bytes", align_bytes=64)
         for quad in range(4):
-            place(nc.sync, k_planes, ks_got, 96, quad)
+            place(nc.sync, k_planes, ks_got, 96, quad, 1)
         nc.vector.tensor_copy(cs_got[:], cs_win[:].indirect(offsets[:]))
         c_planes = pool.tile([P, PASSES, N], U8, name="c_planes", tag="c_bytes", align_bytes=64)
         for quad in range(4):
-            place(nc.sync, c_planes, cs_got, 32, quad)
+            place(nc.sync, c_planes, cs_got, 32, quad, 2)
 
         kw_got = pool.tile([P, N], U32, name="kw_got", align_bytes=64)
         kw = pool.tile([P, PASSES, N], U16, name="kw", align_bytes=64)

@@ -82,7 +82,7 @@ def tile_attend_twokey_topk_kernel(tc, qT, k_words, k_scales, c_words, c_scales,
             q_bf = pool.tile([P, NQ, PACK], BF16, name="q_bf%d" % g, align_bytes=64)
             codes = pool.tile([P, NQ], U32, name="q_codes%d" % g, align_bytes=64)
             scales = pool.tile([P, NQ], U8, name="q_scales%d" % g, align_bytes=64)
-            nc.scalar.activation(q_bf[:], q_raw[:, g].rearrange("p j w -> p w j"), ACT.Copy)
+            nc.scalar.activation(q_bf[:], q_raw[:, g].rearrange("p j w -> p w j"), ACT.Copy, scale=0.5)
             nc.vector.quantize_mx(
                 out=codes[:].bitcast(FP8X4), scales=scales[:], in_=q_bf[:].rearrange("p w j -> p (w j)")
             )
@@ -106,7 +106,7 @@ def tile_attend_twokey_topk_kernel(tc, qT, k_words, k_scales, c_words, c_scales,
             cols = slice(h * HALF, (h + 1) * HALF)
             a_ps = psum.tile([P, HALF], F32, name="a_ps%d" % h)
             product(a_ps[:], kw, k_planes, cols, cols, (0, 1) if h == 0 else (1, 0))
-            nc.scalar.activation(gate[:, cols], a_ps[:], ACT.Sigmoid)
+            nc.scalar.activation(gate[:, cols], a_ps[:], ACT.Tanh)
 
         cw_got = []
         for h in range(2):
@@ -130,5 +130,12 @@ def tile_attend_twokey_topk_kernel(tc, qT, k_words, k_scales, c_words, c_scales,
             y = pool.tile([P, HALF], F32, name="y%d" % h)
             for i in range(2):
                 s = 2 * h + i
-                nc.vector.tensor_tensor(y[:, i * P : (i + 1) * P], z_ps[s][:], gate[:, s * P : (s + 1) * P], ALU.mult)
+                nc.vector.scalar_tensor_tensor(
+                    out=y[:, i * P : (i + 1) * P],
+                    in0=gate[:, s * P : (s + 1) * P],
+                    scalar=1.0,
+                    in1=z_ps[s][:],
+                    op0=ALU.add,
+                    op1=ALU.mult,
+                )
             nc.sync.dma_start(out=out[0][:, h * HALF : (h + 1) * HALF], in_=y[:])

from contextlib import ExitStack

import concourse.mybir as mybir

N, T, D, NQ = 512, 2048, 1024, 128
FLOPS = 2 * 2 * NQ * N * D

F32 = mybir.dt.float32
BF16 = mybir.dt.bfloat16
I32 = mybir.dt.int32
U32 = mybir.dt.uint32
U16 = mybir.dt.uint16
U8 = mybir.dt.uint8
FP8X4 = mybir.dt.float8_e4m3fn_x4
FP4X4 = mybir.dt.float4_e2m1fn_x4
ACT = mybir.ActivationFunctionType
ALU = mybir.AluOpType

P = 128
PACK = 4
PASSES = 2
HALF = N // 2


def tile_attend_twokey_topk_kernel(tc, qT, k_words, k_scales, c_words, c_scales, offs, out):
    nc = tc.nc
    with ExitStack() as ctx:
        pool = ctx.enter_context(tc.tile_pool(name="held", bufs=1))
        psum = ctx.enter_context(tc.psum_pool(name="psum", bufs=1))

        offsets = pool.tile([P, N // 16], U16, name="offsets")
        ks_win = pool.tile([P, T], U8, name="ks_win", tag="k_bytes", align_bytes=64)
        cs_win = pool.tile([P, T], U8, name="cs_win", tag="c_bytes", align_bytes=64)
        cw_win = pool.tile([P, T], I32, name="cw_win", align_bytes=64)
        kw_win = pool.tile([P, T], I32, name="kw_win", align_bytes=64)
        ks_got = pool.tile([P, N], U8, name="ks_got", align_bytes=64)
        cs_got = pool.tile([P, N], U8, name="cs_got", align_bytes=64)

        def load_scales(win, scales, first, blanks, engine):
            rows = scales.rearrange("o f t -> f o t")
            nc.sync.dma_start(out=win[first : first + 32, :].bitcast(I32), in_=rows.bitcast(I32))
            for lo, hi in blanks:
                engine.memset(win[lo:hi, :].bitcast(I32), 0)

        def place(queue, planes, got, first, quad, step):
            queue.dma_start(
                out=planes[32 * quad : 32 * quad + 4].bitcast(I32),
                in_=got[first + 8 * step * quad : first + 8 * step * (quad + 1) : step].bitcast(I32),
            )

        def load_words(win, words):
            nc.sync.dma_start(out=win[:], in_=words[0].rearrange("p t b -> p (t b)").bitcast(I32))

        nc.vector.memset(cs_win[:].bitcast(I32), 0)
        load_scales(ks_win, k_scales, 96, [(0, 96)], nc.vector)
        nc.sync.dma_start(offsets[:], offs)
        q_raw = pool.tile([P, PASSES, PACK, NQ], F32, name="q_raw")
        nc.sync.dma_start(out=q_raw[:], in_=qT[0].rearrange("(g p j) w -> p g j w", g=PASSES, j=PACK))
        nc.sync.dma_start(
            out=cs_win[32:96:2, :].bitcast(I32), in_=c_scales.rearrange("o f t -> f o t").bitcast(I32)
        )
        load_words(kw_win, k_words)
        load_words(cw_win, c_words)

        nc.vector.tensor_copy(ks_got[:], ks_win[:].indirect(offsets[:]))
        k_planes = pool.tile([P, PASSES, N], U8, name="k_planes", tag="k_bytes", align_bytes=64)
        for quad in range(4):
            place(nc.sync, k_planes, ks_got, 96, quad, 1)
        nc.vector.tensor_copy(cs_got[:], cs_win[:].indirect(offsets[:]))
        c_planes = pool.tile([P, PASSES, N], U8, name="c_planes", tag="c_bytes", align_bytes=64)
        for quad in range(4):
            place(nc.sync, c_planes, cs_got, 32, quad, 2)

        kw_got = pool.tile([P, N], U32, name="kw_got", align_bytes=64)
        kw = pool.tile([P, PASSES, N], U16, name="kw", align_bytes=64)
        nc.vector.tensor_copy(kw_got[:], kw_win[:].bitcast(U32).indirect(offsets[:]))
        for g in range(PASSES):
            nc.vector.tensor_copy(kw[:, g], kw_got[:].bitcast(U16).rearrange("p (n g) -> p g n", g=PASSES)[:, g])

        q_codes, q_scales = [], []
        for g in range(PASSES):
            q_bf = pool.tile([P, NQ, PACK], BF16, name="q_bf%d" % g, align_bytes=64)
            codes = pool.tile([P, NQ], U32, name="q_codes%d" % g, align_bytes=64)
            scales = pool.tile([P, NQ], U8, name="q_scales%d" % g, align_bytes=64)
            nc.scalar.activation(q_bf[:], q_raw[:, g].rearrange("p j w -> p w j"), ACT.Copy, scale=0.5)
            nc.vector.quantize_mx(
                out=codes[:].bitcast(FP8X4), scales=scales[:], in_=q_bf[:].rearrange("p w j -> p (w j)")
            )
            q_codes.append(codes)
            q_scales.append(scales)

        def product(acc, words, planes, cols, wcols, order):
            for g in order:
                nc.tensor.matmul_mx(
                    out=acc,
                    lhsT=q_codes[g][:].bitcast(FP8X4),
                    lhsT_scale=q_scales[g][:],
                    rhs=words[:, g, wcols].bitcast(FP4X4),
                    rhs_scale=planes[:, g, cols],
                    start=(g == order[0]),
                    stop=(g == order[-1]),
                )

        gate = pool.tile([P, N], F32, name="gate")
        for h in range(2):
            cols = slice(h * HALF, (h + 1) * HALF)
            a_ps = psum.tile([P, HALF], F32, name="a_ps%d" % h)
            product(a_ps[:], kw, k_planes, cols, cols, (0, 1) if h == 0 else (1, 0))
            nc.scalar.activation(gate[:, cols], a_ps[:], ACT.Tanh)

        cw_got = []
        for h in range(2):
            got = pool.tile([P, HALF], U32, name="cw_got%d" % h, align_bytes=64)
            nc.vector.tensor_copy(got[:], cw_win[:].bitcast(U32).indirect(offsets[:, h * 16 : (h + 1) * 16]))
            cw_got.append(got)

        z_ps = [psum.tile([P, P], F32, name="z_ps%d" % s) for s in range(4)]
        for s in range(4):
            cw = pool.tile([P, PASSES, P], U16, name="cw%d" % s, align_bytes=64)
            src = cw_got[s // 2][:, (s % 2) * P : (s % 2 + 1) * P].bitcast(U16)
            halves = src.rearrange("p (n g) -> p g n", g=PASSES)
            if s in (0, 3):
                for g in (0, 1) if s == 0 else (1, 0):
                    nc.vector.tensor_copy(cw[:, g], halves[:, g])
            else:
                nc.vector.tensor_copy(cw[:], halves)
            product(z_ps[s][:], cw, c_planes, slice(s * P, (s + 1) * P), slice(0, P), (0, 1) if s % 2 == 0 else (1, 0))

        for h in range(2):
            y = pool.tile([P, HALF], F32, name="y%d" % h)
            for i in range(2):
                s = 2 * h + i
                nc.vector.scalar_tensor_tensor(
                    out=y[:, i * P : (i + 1) * P],
                    in0=gate[:, s * P : (s + 1) * P],
                    scalar=1.0,
                    in1=z_ps[s][:],
                    op0=ALU.add,
                    op1=ALU.mult,
                )
            nc.sync.dma_start(out=out[0][:, h * HALF : (h + 1) * HALF], in_=y[:])
